import numpy as np
CORES = [0,1,2,3,4,5,6,7]
N = 8
WIDTHS = [1024,8,8,8,512,8,8,8]
XW = 1024
def setup_inputs(rng):
    return {"x": rng.standard_normal((N, 128, XW), dtype=np.float32)}
def reference(x):
    g = np.concatenate([x[r][:, :WIDTHS[r]] for r in range(N)], axis=1)
    return {"y": np.broadcast_to(g, (N,) + g.shape)}

@@ -1,0 +1,36 @@
+from concourse.bass import DstId, RemoteDMATransfer
+
+TOTAL = 1584
+
+SCRATCH = {
+    "land": ("sbuf", [128, TOTAL], "float32"),
+}
+SEMAPHORES = ["loaded", "arrived", "stored"]
+
+
+def rank_program(g, core, T, topo):
+    rank = T.rank_of(core)
+    if rank is None:
+        return
+    widths = T.tables["WIDTHS"]
+    n = len(widths)
+    off = [sum(widths[:r]) for r in range(n)]
+    w = widths[rank]
+    mine = T.land[:, off[rank]:off[rank] + w]
+
+    g.sync.dma_start(mine, T.x[:, 0:w]).then_inc(T.sem.loaded, 16)
+    g.wait_ge(T.sem.loaded, 16)
+
+    peers = [c for c in T.cores if c != core]
+    ids = []
+    for c in peers:
+        rid, pid, _se = topo.addr(c)
+        ids.append(DstId(rid=rid, pnc=pid))
+    g.remote_dma_fused(
+        [RemoteDMATransfer(dst_ids=ids, dma_engine_mask=0xFFFF, remote_sem=T.sem.arrived,
+                           srcs=[mine], dsts=[mine for _c in peers], alu_op=0)],
+        local_sem=T.sem.arrived)
+
+    g.wait_ge(T.sem.arrived, 16 * n)
+    g.dma_start(T.y[:, :], T.land[:, :]).then_inc(T.sem.stored, 16)
+    g.wait_ge(T.sem.stored, 16)

@@ -1,11 +1,21 @@
 from concourse.bass import DstId, RemoteDMATransfer
 
-TOTAL = 1584
+ALL = 0xFFFF
+ROUNDS = 3
+L_ROWS, L_SLOTS = 6, 21
+M_ROWS, M_SLOTS = 8, 16
 
 SCRATCH = {
-    "land": ("sbuf", [128, TOTAL], "float32"),
+    "L": ("dram", [L_SLOTS, 128, 48], "float32"),
+    "Lt": ("dram", [2, 128, 8], "float32"),
+    "M": ("dram", [M_SLOTS, 128, 32], "float32"),
+    "st": ("sbuf", [128, 8], "float32"),
+    "gs": ("sbuf", [128, 48], "float32"),
+    "gd": ("dram", [128, 48], "float32"),
 }
-SEMAPHORES = ["loaded", "arrived", "stored"]
+SEMAPHORES = (["cp0", "cp1", "cp2", "ld", "gin", "gcp", "garr", "sent", "stored", "ownLt"]
+              + ["ownL%d" % k for k in range(ROUNDS)] + ["arrL%d" % k for k in range(ROUNDS)]
+              + ["ownM%d" % k for k in range(ROUNDS)] + ["arrM%d" % k for k in range(ROUNDS)])
 
 
 def rank_program(g, core, T, topo):
@@ -15,22 +25,155 @@ def rank_program(g, core, T, topo):
     widths = T.tables["WIDTHS"]
     n = len(widths)
     off = [sum(widths[:r]) for r in range(n)]
-    w = widths[rank]
-    mine = T.land[:, off[rank]:off[rank] + w]
+    BIG, MID = 0, 4
+    WL, WM = widths[BIG], widths[MID]
+    narrow = [r for r in range(n) if r not in (BIG, MID)]
+    AGG = narrow[-1]
+    l_relays = [r for r in range(n) if r != BIG]
+    m_relays = [r for r in narrow if r != AGG]
+    tail_relays = [MID, AGG]
+    nl, nm = len(l_relays), len(m_relays)
+    sem = T.sem
+    sent = [0]
+    stored = [0]
 
-    g.sync.dma_start(mine, T.x[:, 0:w]).then_inc(T.sem.loaded, 16)
-    g.wait_ge(T.sem.loaded, 16)
+    def dst(r):
+        rid, pid, _se = topo.addr(T.cores[r])
+        return DstId(rid=rid, pnc=pid)
 
-    peers = [c for c in T.cores if c != core]
-    ids = []
-    for c in peers:
-        rid, pid, _se = topo.addr(c)
-        ids.append(DstId(rid=rid, pnc=pid))
-    g.remote_dma_fused(
-        [RemoteDMATransfer(dst_ids=ids, dma_engine_mask=0xFFFF, remote_sem=T.sem.arrived,
-                           srcs=[mine], dsts=[mine for _c in peers], alu_op=0)],
-        local_sem=T.sem.arrived)
+    def send(ap, r, remote_sem):
+        rid, pid, _se = topo.addr(T.cores[r])
+        g.remote_dma(ap, ap, remote_sem, sem.sent, pid, rid, ALL)
+        sent[0] += 16
 
-    g.wait_ge(T.sem.arrived, 16 * n)
-    g.dma_start(T.y[:, :], T.land[:, :]).then_inc(T.sem.stored, 16)
-    g.wait_ge(T.sem.stored, 16)
+    def forward(ap, ranks, remote_sem):
+        g.remote_dma_fused(
+            [RemoteDMATransfer(dst_ids=[dst(r) for r in ranks], dma_engine_mask=ALL, remote_sem=remote_sem,
+                               srcs=[ap], dsts=[ap for _r in ranks], alu_op=0)],
+            local_sem=sem.sent)
+        sent[0] += 16
+
+    def store(q, out, in_):
+        q.dma_start(out, in_).then_inc(sem.stored, 16)
+        stored[0] += 16
+
+    def m_slots(k):
+        return nm * k, (nm * (k + 1) if k < ROUNDS - 1 else M_SLOTS)
+
+    def l_others(r):
+        return [d for d in range(n) if d not in (BIG, r)]
+
+    def m_others(r):
+        return [d for d in range(n) if d not in (MID, r)]
+
+    if rank == BIG:
+        for k in range(ROUNDS):
+            r0 = nl * L_ROWS * k
+            g.sync.dma_start(T.L[nl * k:nl * (k + 1)], T.x[r0:r0 + nl * L_ROWS, 0:WL]).then_inc(sem["cp%d" % k], 16)
+        g.sync.dma_start(T.Lt[:], T.x[L_SLOTS * L_ROWS:128, 0:WL]).then_inc(sem.cp2, 16)
+    elif rank == MID:
+        for k in range(ROUNDS):
+            a, b = m_slots(k)
+            g.sync.dma_start(T.M[a:b], T.x[M_ROWS * a:M_ROWS * b, 0:WM]).then_inc(sem["cp%d" % k], 16)
+    else:
+        i = narrow.index(rank)
+        mine = T.gs[:, 8 * i:8 * i + 8] if rank == AGG else T.st[:, :]
+        g.scalar.dma_start(mine, T.x[:, 0:widths[rank]]).then_inc(sem.ld, 16)
+
+    def fwd_l(k):
+        g.wait_ge(sem["ownL%d" % k], 16)
+        forward(T.L[nl * k + l_relays.index(rank)], l_others(rank), sem["arrL%d" % k])
+
+    def fwd_tail():
+        g.wait_ge(sem.ownLt, 16)
+        forward(T.Lt[tail_relays.index(rank)], l_others(rank), sem["arrL%d" % (ROUNDS - 1)])
+
+    def fwd_m(k, slot):
+        g.wait_ge(sem["ownM%d" % k], 16)
+        forward(T.M[slot], m_others(rank), sem["arrM%d" % k])
+
+    if rank == BIG:
+        for k in range(ROUNDS):
+            g.wait_ge(sem["cp%d" % k], 32 if k == ROUNDS - 1 else 16)
+            for i, r in enumerate(l_relays):
+                send(T.L[nl * k + i], r, sem["ownL%d" % k])
+        for i, r in enumerate(tail_relays):
+            send(T.Lt[i], r, sem.ownLt)
+    elif rank == MID:
+        for k in range(ROUNDS):
+            g.wait_ge(sem["cp%d" % k], 16)
+            for i, r in enumerate(m_relays):
+                send(T.M[nm * k + i], r, sem["ownM%d" % k])
+        send(T.M[M_SLOTS - 1], AGG, sem["ownM%d" % (ROUNDS - 1)])
+        for k in range(ROUNDS):
+            fwd_l(k)
+        fwd_tail()
+    elif rank == AGG:
+        g.scalar.wait_ge(sem.ld, 16)
+        g.scalar.wait_ge(sem.gin, 16 * (len(narrow) - 1))
+        g.scalar.dma_start(T.gd[:, :], T.gs[:, :]).then_inc(sem.gcp, 16)
+        g.wait_ge(sem.gcp, 16)
+        forward(T.gd[:, :], [d for d in range(n) if d != rank], sem.garr)
+        fwd_l(0)
+        fwd_m(ROUNDS - 1, M_SLOTS - 1)
+        fwd_l(1)
+        fwd_l(2)
+        fwd_tail()
+    else:
+        g.wait_ge(sem.ld, 16)
+        i = narrow.index(rank)
+        rid, pid, _se = topo.addr(T.cores[AGG])
+        g.remote_dma(T.gs[:, 8 * i:8 * i + 8], T.st[:, :], sem.gin, sem.sent, pid, rid, ALL)
+        sent[0] += 16
+        j = m_relays.index(rank)
+        fwd_m(0, j)
+        fwd_l(0)
+        fwd_m(1, nm + j)
+        fwd_m(2, 2 * nm + j)
+        fwd_l(1)
+        fwd_l(2)
+
+    q = g.sync
+    if rank == AGG:
+        q.wait_ge(sem.ld, 16)
+        q.wait_ge(sem.gin, 16 * (len(narrow) - 1))
+        gsrc = T.gs
+    else:
+        q.wait_ge(sem.garr, 16)
+        gsrc = T.gd
+    store(q, T.y[:, off[1]:off[4]], gsrc[:, 0:24])
+    store(q, T.y[:, off[5]:off[7] + widths[7]], gsrc[:, 24:48])
+
+    if rank == BIG:
+        g.scalar.wait_ge(sem.cp2, 32)
+        store(g.scalar, T.y[:, 0:WL], T.x[:, 0:WL])
+    else:
+        for k in range(ROUNDS):
+            last = k == ROUNDS - 1
+            q.wait_ge(sem["ownL%d" % k], 16)
+            arr = 16 * (nl - 1)
+            if last:
+                arr += 16 * len([r for r in tail_relays if r != rank])
+                if rank in tail_relays:
+                    q.wait_ge(sem.ownLt, 16)
+            q.wait_ge(sem["arrL%d" % k], arr)
+            r0 = nl * L_ROWS * k
+            store(q, T.y[r0:r0 + nl * L_ROWS, 0:WL], T.L[nl * k:nl * (k + 1)])
+            if last:
+                store(q, T.y[L_SLOTS * L_ROWS:128, 0:WL], T.Lt[:])
+
+    q = g.scalar
+    if rank == MID:
+        q.wait_ge(sem.cp2, 16)
+        store(q, T.y[:, off[MID]:off[MID] + WM], T.x[:, 0:WM])
+    else:
+        for k in range(ROUNDS):
+            a, b = m_slots(k)
+            mine = 1 if (rank in m_relays or (rank == AGG and k == ROUNDS - 1)) else 0
+            if mine:
+                q.wait_ge(sem["ownM%d" % k], 16)
+            q.wait_ge(sem["arrM%d" % k], 16 * (b - a - mine))
+            store(q, T.y[M_ROWS * a:M_ROWS * b, off[MID]:off[MID] + WM], T.M[a:b])
+
+    g.wait_ge(sem.sent, sent[0])
+    g.wait_ge(sem.stored, stored[0])

from concourse.bass import DstId, RemoteDMATransfer

ALL = 0xFFFF
ROUNDS = 3
L_ROWS, L_SLOTS = 6, 21
M_ROWS, M_SLOTS = 8, 16

SCRATCH = {
    "L": ("dram", [L_SLOTS, 128, 48], "float32"),
    "Lt": ("dram", [2, 128, 8], "float32"),
    "M": ("dram", [M_SLOTS, 128, 32], "float32"),
    "st": ("sbuf", [128, 8], "float32"),
    "gs": ("sbuf", [128, 48], "float32"),
    "gd": ("dram", [128, 48], "float32"),
}
SEMAPHORES = (["cp0", "cp1", "cp2", "ld", "gin", "gcp", "garr", "sent", "stored", "ownLt"]
              + ["ownL%d" % k for k in range(ROUNDS)] + ["arrL%d" % k for k in range(ROUNDS)]
              + ["ownM%d" % k for k in range(ROUNDS)] + ["arrM%d" % k for k in range(ROUNDS)])


def rank_program(g, core, T, topo):
    rank = T.rank_of(core)
    if rank is None:
        return
    widths = T.tables["WIDTHS"]
    n = len(widths)
    off = [sum(widths[:r]) for r in range(n)]
    BIG, MID = 0, 4
    WL, WM = widths[BIG], widths[MID]
    narrow = [r for r in range(n) if r not in (BIG, MID)]
    AGG = narrow[-1]
    l_relays = [r for r in range(n) if r != BIG]
    m_relays = [r for r in narrow if r != AGG]
    tail_relays = [MID, AGG]
    nl, nm = len(l_relays), len(m_relays)
    sem = T.sem
    sent = [0]
    stored = [0]

    def dst(r):
        rid, pid, _se = topo.addr(T.cores[r])
        return DstId(rid=rid, pnc=pid)

    def send(ap, r, remote_sem):
        rid, pid, _se = topo.addr(T.cores[r])
        g.remote_dma(ap, ap, remote_sem, sem.sent, pid, rid, ALL)
        sent[0] += 16

    def forward(ap, ranks, remote_sem):
        g.remote_dma_fused(
            [RemoteDMATransfer(dst_ids=[dst(r) for r in ranks], dma_engine_mask=ALL, remote_sem=remote_sem,
                               srcs=[ap], dsts=[ap for _r in ranks], alu_op=0)],
            local_sem=sem.sent)
        sent[0] += 16

    def store(q, out, in_):
        q.dma_start(out, in_).then_inc(sem.stored, 16)
        stored[0] += 16

    def m_slots(k):
        return nm * k, (nm * (k + 1) if k < ROUNDS - 1 else M_SLOTS)

    def l_others(r):
        return [d for d in range(n) if d not in (BIG, r)]

    def m_others(r):
        return [d for d in range(n) if d not in (MID, r)]

    if rank == BIG:
        for k in range(ROUNDS):
            r0 = nl * L_ROWS * k
            g.sync.dma_start(T.L[nl * k:nl * (k + 1)], T.x[r0:r0 + nl * L_ROWS, 0:WL]).then_inc(sem["cp%d" % k], 16)
        g.sync.dma_start(T.Lt[:], T.x[L_SLOTS * L_ROWS:128, 0:WL]).then_inc(sem.cp2, 16)
    elif rank == MID:
        for k in range(ROUNDS):
            a, b = m_slots(k)
            g.sync.dma_start(T.M[a:b], T.x[M_ROWS * a:M_ROWS * b, 0:WM]).then_inc(sem["cp%d" % k], 16)
    else:
        i = narrow.index(rank)
        mine = T.gs[:, 8 * i:8 * i + 8] if rank == AGG else T.st[:, :]
        g.scalar.dma_start(mine, T.x[:, 0:widths[rank]]).then_inc(sem.ld, 16)

    def fwd_l(k):
        g.wait_ge(sem["ownL%d" % k], 16)
        forward(T.L[nl * k + l_relays.index(rank)], l_others(rank), sem["arrL%d" % k])

    def fwd_tail():
        g.wait_ge(sem.ownLt, 16)
        forward(T.Lt[tail_relays.index(rank)], l_others(rank), sem["arrL%d" % (ROUNDS - 1)])

    def fwd_m(k, slot):
        g.wait_ge(sem["ownM%d" % k], 16)
        forward(T.M[slot], m_others(rank), sem["arrM%d" % k])

    if rank == BIG:
        for k in range(ROUNDS):
            g.wait_ge(sem["cp%d" % k], 32 if k == ROUNDS - 1 else 16)
            for i, r in enumerate(l_relays):
                send(T.L[nl * k + i], r, sem["ownL%d" % k])
        for i, r in enumerate(tail_relays):
            send(T.Lt[i], r, sem.ownLt)
    elif rank == MID:
        for k in range(ROUNDS):
            g.wait_ge(sem["cp%d" % k], 16)
            for i, r in enumerate(m_relays):
                send(T.M[nm * k + i], r, sem["ownM%d" % k])
        send(T.M[M_SLOTS - 1], AGG, sem["ownM%d" % (ROUNDS - 1)])
        for k in range(ROUNDS):
            fwd_l(k)
        fwd_tail()
    elif rank == AGG:
        g.scalar.wait_ge(sem.ld, 16)
        g.scalar.wait_ge(sem.gin, 16 * (len(narrow) - 1))
        g.scalar.dma_start(T.gd[:, :], T.gs[:, :]).then_inc(sem.gcp, 16)
        g.wait_ge(sem.gcp, 16)
        forward(T.gd[:, :], [d for d in range(n) if d != rank], sem.garr)
        fwd_l(0)
        fwd_m(ROUNDS - 1, M_SLOTS - 1)
        fwd_l(1)
        fwd_l(2)
        fwd_tail()
    else:
        g.wait_ge(sem.ld, 16)
        i = narrow.index(rank)
        rid, pid, _se = topo.addr(T.cores[AGG])
        g.remote_dma(T.gs[:, 8 * i:8 * i + 8], T.st[:, :], sem.gin, sem.sent, pid, rid, ALL)
        sent[0] += 16
        j = m_relays.index(rank)
        fwd_m(0, j)
        fwd_l(0)
        fwd_m(1, nm + j)
        fwd_m(2, 2 * nm + j)
        fwd_l(1)
        fwd_l(2)

    q = g.sync
    if rank == AGG:
        q.wait_ge(sem.ld, 16)
        q.wait_ge(sem.gin, 16 * (len(narrow) - 1))
        gsrc = T.gs
    else:
        q.wait_ge(sem.garr, 16)
        gsrc = T.gd
    store(q, T.y[:, off[1]:off[4]], gsrc[:, 0:24])
    store(q, T.y[:, off[5]:off[7] + widths[7]], gsrc[:, 24:48])

    if rank == BIG:
        g.scalar.wait_ge(sem.cp2, 32)
        store(g.scalar, T.y[:, 0:WL], T.x[:, 0:WL])
    else:
        for k in range(ROUNDS):
            last = k == ROUNDS - 1
            q.wait_ge(sem["ownL%d" % k], 16)
            arr = 16 * (nl - 1)
            if last:
                arr += 16 * len([r for r in tail_relays if r != rank])
                if rank in tail_relays:
                    q.wait_ge(sem.ownLt, 16)
            q.wait_ge(sem["arrL%d" % k], arr)
            r0 = nl * L_ROWS * k
            store(q, T.y[r0:r0 + nl * L_ROWS, 0:WL], T.L[nl * k:nl * (k + 1)])
            if last:
                store(q, T.y[L_SLOTS * L_ROWS:128, 0:WL], T.Lt[:])

    q = g.scalar
    if rank == MID:
        q.wait_ge(sem.cp2, 16)
        store(q, T.y[:, off[MID]:off[MID] + WM], T.x[:, 0:WM])
    else:
        for k in range(ROUNDS):
            a, b = m_slots(k)
            mine = 1 if (rank in m_relays or (rank == AGG and k == ROUNDS - 1)) else 0
            if mine:
                q.wait_ge(sem["ownM%d" % k], 16)
            q.wait_ge(sem["arrM%d" % k], 16 * (b - a - mine))
            store(q, T.y[M_ROWS * a:M_ROWS * b, off[MID]:off[MID] + WM], T.M[a:b])

    g.wait_ge(sem.sent, sent[0])
    g.wait_ge(sem.stored, stored[0])
